import numpy as np, ml_dtypes
CORES = [1,17,65,89,97,113]
N = 6
R, T, B = 16384, 4096, 256
def entries(a): return a.T.reshape(-1)
def pack(v, P): return np.ascontiguousarray(np.asarray(v, np.int32).reshape(-1, P).T)
def lists(rng, how):
    I = rng.integers(0, N * R, (N, T)); E = np.sort(rng.integers(0, T + 1, (N, B)), axis=1)
    if how == "void":
        E = np.zeros((N, B), np.int64)
        for r in range(N): k = np.sort(1 + rng.permutation(B - 2)[:6]); c = np.sort(1 + rng.permutation(T)[:6]); E[r] = np.concatenate([[0], c])[np.searchsorted(k, np.arange(B), side="right")]
        E[rng.integers(N)] = 0
    if how == "one":
        p = rng.permutation(N); z = rng.integers(0, B, N); z[p[0]] = 0; z[p[1]] = B - 1; E = np.where(np.arange(B)[None, :] < z[:, None], 0, T)
        I[p[::2]] = R * p[1] + I[p[::2]] % R
    if how == "single": E = np.broadcast_to(1 + np.arange(B), (N, B)).copy()
    if how == "hotrank": I = R * int(rng.integers(N)) + rng.integers(0, R, (N, T))
    if how == "edge": I = R * rng.integers(0, N, (N, T)) + np.where(rng.random((N, T)) < 0.5, 0, R - 1); E[:, -1] = T
    return {"idx": np.stack([pack(i, 16) for i in I]), "end": np.stack([pack(v, 16) for v in E])}
def setup_inputs(rng):
    return dict({"tab": rng.standard_normal((N, 128, R), dtype=np.float32).astype(ml_dtypes.bfloat16)}, **lists(rng, "uniform"))
def setup_inputs_edge(rng):
    d = setup_inputs(rng); d.update(lists(rng, "edge"))
    for k in ("tab",): d[k] = (d[k].astype(np.float32) * 1048576.0).astype(d[k].dtype)
    return d
def setup_inputs_hotrank(rng):
    d = setup_inputs(rng); d.update(lists(rng, "hotrank"))
    for k in ("tab",): d[k] = (d[k].astype(np.float32) * (1 / 1024.0)).astype(d[k].dtype)
    return d
def setup_inputs_one(rng):
    d = setup_inputs(rng); d.update(lists(rng, "one"))
    return d
def setup_inputs_single(rng):
    d = setup_inputs(rng); d.update(lists(rng, "single"))
    return d
def setup_inputs_void(rng):
    d = setup_inputs(rng); d.update(lists(rng, "void"))
    return d
def check_inputs(x):
    bad = []
    if x["idx"].min() < 0 or x["idx"].max() >= N * R: bad.append("idx out of range")
    if x["end"].min() < 0 or x["end"].max() >= T + 1: bad.append("end out of range")
    if any((np.diff(entries(a)) < 0).any() for a in x["end"]): bad.append("end falls")
    t = x["tab"].astype(np.float32)
    if t.min() < -1e30 or t.max() > 1e30: bad.append("tab beyond -1e30 to 1e30")
    return bad
def reference(tab, idx, end):
    A = np.concatenate(list(tab), axis=1)
    y = np.zeros((N, 128, B), tab.dtype)
    for r in range(N):
        G = A[:, entries(idx[r])]; c = np.concatenate([[0], entries(end[r])])
        for b in range(B):
            if c[b + 1] > c[b]: y[r][:, b] = G[:, c[b]:c[b + 1]].max(axis=1)
    return {"y": y}

@@ -1,0 +1,364 @@
+import numpy as np
+from concourse.bass import DstId, RemoteDMATransfer
+from concourse.mybir import AluOpType as A, ActivationFunctionType as F
+
+NR, R, TT, B = 6, 16384, 4096, 256
+PK = 256 + 32
+LO = 8
+W = LO + R + 8
+MAXJ = 3
+ROUNDS = (2560, 1792)
+MULTI = (1280, (1408, 1408))
+SINGLE = (1536, (1280, 1280))
+
+SCRATCH = {
+    "ix": ("sbuf", [16, 256], "int32"), "en": ("sbuf", [16, 16], "int32"),
+    "idf": ("sbuf", [16, 256], "float32"), "enf": ("sbuf", [16, 32], "float32"),
+    "ones": ("sbuf", [16, 128], "float32"),
+    "selr": ("sbuf", [16, 128], "float32"), "sels": ("sbuf", [16, 128], "float32"), "selw": ("sbuf", [16, 128], "float32"),
+    "di": ("sbuf", [128, 16], "int32"), "dm": ("sbuf", [128, 16], "int32"), "dc": ("sbuf", [128, 16], "int32"),
+    "zc": ("sbuf", [128, 32], "float32"), "yc": ("sbuf", [128, 32], "float32"),
+    "xx": ("sbuf", [128, 32], "float32"), "ne": ("sbuf", [128, 32], "float32"),
+    "w1": ("sbuf", [128, 32], "float32"), "w2": ("sbuf", [128, 32], "float32"), "w3": ("sbuf", [128, 32], "float32"),
+    "pk": ("sbuf", [128, NR * PK], "uint16"), "rb": ("sbuf", [128, NR * PK], "uint16"),
+    "nega": ("sbuf", [128, 256], "bfloat16"), "negb": ("sbuf", [128, 256], "bfloat16"),
+    "tb": ("sbuf", [128, W], "bfloat16"), "yb": ("sbuf", [128, B], "bfloat16"),
+    "pse": ("psum", [128, 512], "float32"), "psi": ("psum", [128, 512], "float32"), "acc": ("psum", [128, 512], "float32"),
+}
+for _j in range(MAXJ):
+    SCRATCH["rq%d" % _j] = ("sbuf", [128, PK], "uint16")
+    SCRATCH["mk%d" % _j] = ("sbuf", [128, TT + B], "bfloat16")
+    SCRATCH["ga%d" % _j] = ("sbuf", [128, TT], "bfloat16")
+    SCRATCH["so%d" % _j] = ("sbuf", [128, 8 + TT], "bfloat16")
+    SCRATCH["po%d" % _j] = ("sbuf", [128, B], "bfloat16")
+    SCRATCH["rr%d" % _j] = ("sbuf", [128, B], "bfloat16")
+for _r in range(NR):
+    SCRATCH["pt%d" % _r] = ("sbuf", [128, B], "bfloat16")
+SEMAPHORES = (["ldi", "ldt0", "ldt1", "vv", "c1", "gl", "gi", "vc", "pe1", "pe2", "sn", "loc", "yv", "yst", "rl",
+               "tco0", "tco1", "tco2", "tcf"]
+              + ["k%d" % r for r in range(NR)] + ["pt%d" % r for r in range(NR)]
+              + [n + str(j) for j in range(MAXJ) for n in ("rq", "rr", "ex", "sa", "sb")])
+
+
+def pop(m):
+    return bin(m).count("1")
+
+
+def split(mask, n):
+    bits = [b for b in range(32) if mask >> b & 1]
+    k = 1
+    while 2 * k * n <= len(bits):
+        k *= 2
+    return [sum(1 << b for b in bits[i * k:(i + 1) * k]) for i in range(n)]
+
+
+def plan(T, topo):
+    every = range(topo.CORES_PER_CHIP * topo.CHIPS)
+    P = {"help": [], "relay": [], "jobs": {}, "at": {}, "ret": {}, "reqrelay": {}, "peers": [], "far": []}
+    cores = [int(c) for c in T.cores]
+    P["cores"] = cores
+    for r in range(NR):
+        own = [c for c in every if topo.chip(c) == topo.chip(cores[r])]
+        other = [c for c in every if topo.mates(topo.chip(c), topo.chip(cores[r]))][0]
+        port = [c for c in own if topo.may_write(c, other)]
+        mine = [c for c in own if topo.die(c) == topo.die(cores[r]) and c != cores[r]]
+        P["help"].append([c for c in mine if c in port] + [c for c in mine if c not in port])
+        P["relay"].append([c for c in port if topo.die(c) != topo.die(cores[r])])
+        P["peers"].append([s for s in range(NR) if s != r and topo.may_write(cores[r], cores[s])])
+        P["far"].append([s for s in range(NR) if s != r and not topo.may_write(cores[r], cores[s])])
+    for s in range(NR):
+        h, peers, far = P["help"][s], P["peers"][s], P["far"][s]
+        near = [p for p in peers if p > s] + [p for p in peers if p < s]
+        if len(far) <= 1:
+            take = {cores[s]: [s] + near[0:2], h[0]: far, h[1]: near[2:3], h[2]: near[3:4]}
+        else:
+            take = {cores[s]: far[2:], h[0]: far[0:1], h[1]: far[1:2], h[2]: [s]}
+        for c in take:
+            P["jobs"][c] = (s, take[c])
+            for j, r in enumerate(take[c]):
+                P["at"][s, r] = (c, j)
+    for r in range(NR):
+        runs = []
+        for s in P["far"][r]:
+            if runs and runs[-1][-1] == s - 1:
+                runs[-1].append(s)
+            else:
+                runs.append([s])
+        P["reqrelay"][r] = [(P["relay"][r][i % 2], run) for i, run in enumerate(runs)]
+    for s in range(NR):
+        for i, r in enumerate([r for r in P["jobs"][cores[s]][1] if r != s and not topo.may_write(cores[s], cores[r])]):
+            P["ret"][s, r] = (P["relay"][s][i % 2], i // 2)
+    P["rqmask"] = {}
+    for r in range(NR):
+        direct = [s for s in P["peers"][r]]
+        if direct:
+            ms = split(min(topo.mask(cores[r], P["at"][s, r][0]) for s in direct), len(direct))
+            for s, m in zip(direct, ms):
+                P["rqmask"][s, r] = m
+        for rc, run in P["reqrelay"][r]:
+            ms = split(topo.mask(rc, P["at"][run[0], r][0]), len(run))
+            for s, m in zip(run, ms):
+                P["rqmask"][s, r] = m
+        if P["at"][r, r][0] != cores[r]:
+            P["rqmask"][r, r] = topo.mask(cores[r], P["at"][r, r][0])
+    return P
+
+
+def chunks():
+    out, c = [], LO
+    left = R - 3 * sum(ROUNDS)
+    last = [left // 24 * 8] * 3
+    last[0] += left - sum(last)
+    for k in range(3):
+        for h in range(3):
+            w = ROUNDS[k] if k < 2 else last[h]
+            out.append((c, c + w, h, k))
+            c += w
+    return out
+
+
+def rank_program(g, core, T, topo):
+    P = plan(T, topo)
+    cores = P["cores"]
+    rank = T.rank_of(core)
+    S = T.sem
+    cnt = {"vv": 0, "loc": 0}
+    V, SC = g.vector, g.scalar
+
+    def v(ins):
+        ins.then_inc(S.vv, 1)
+        cnt["vv"] += 1
+
+    def vw():
+        if cnt["vv"]:
+            V.wait_ge(S.vv, cnt["vv"])
+
+    def send(dst, out, in_, sem, m=None):
+        m = topo.mask(core, dst) if m is None else m
+        rid, pid, _ = topo.addr(dst)
+        g.remote_dma(out, in_, S[sem], S.loc, pid, rid, m)
+        cnt["loc"] += pop(m)
+
+    def fused(items):
+        tr = []
+        for dsts, out, in_, sem, m in items:
+            ids = []
+            for d in dsts:
+                rid, pid, _ = topo.addr(d)
+                ids.append(DstId(rid=rid, pnc=pid))
+            tr.append(RemoteDMATransfer(dst_ids=ids, dma_engine_mask=m, remote_sem=S[sem], srcs=[in_],
+                                        dsts=[out for _ in dsts], alu_op=0))
+            cnt["loc"] += pop(m)
+        g.remote_dma_fused(tr, local_sem=S.loc)
+
+    for r in range(NR):
+        if core in P["relay"][r]:
+            for rc, run in P["reqrelay"][r]:
+                if rc == core:
+                    g.wait_ge(S.rl, pop(topo.mask(cores[r], core)))
+                    items = []
+                    for i, s in enumerate(run):
+                        hc, j = P["at"][s, r]
+                        items.append(([hc], T["rq%d" % j][:], T.rb[:, i * PK:(i + 1) * PK], "rq%d" % j, P["rqmask"][s, r]))
+                    fused(items)
+            for q in P["jobs"][cores[r]][1]:
+                if P["ret"].get((r, q), (None, 0))[0] == core:
+                    i = P["ret"][r, q][1]
+                    g.wait_ge(S["rr%d" % i], pop(topo.mask(cores[r], core)))
+                    send(cores[q], T["pt%d" % r][:], T["rr%d" % i][:], "pt%d" % r)
+    if core not in P["jobs"]:
+        if cnt["loc"]:
+            g.wait_ge(S.loc, cnt["loc"])
+        return
+
+    s, jobs = P["jobs"][core]
+    ch = chunks()
+    helpers = P["help"][s]
+
+    def pkt(j):
+        r = jobs[j]
+        if rank is not None and r == rank:
+            return T.pk, rank * PK, S["k%d" % rank], 2
+        return T["rq%d" % j], 0, S["rq%d" % j], pop(P["rqmask"][s, r])
+
+    if rank is not None:
+        g.sync.dma_start(T.ix[:], T.idx[:]).then_inc(S.ldi, 16)
+        SC.dma_start(T.en[:], T.end[:]).then_inc(S.ldi, 16)
+        cut = ch[6][0]
+        g.sync.dma_start(T.tb[:, LO:cut], T.tab[:, 0:cut - LO]).then_inc(S.ldt0, 16)
+        g.sync.dma_start(T.tb[:, cut:LO + R], T.tab[:, cut - LO:R]).then_inc(S.ldt1, 16)
+        g.iota(T.di[:], [[0, 16]], 0, 1).then_inc(S.gi, 1)
+        g.iota(T.dc[:], [[16, 16]], TT, 0).then_inc(S.gi, 1)
+        V.memset(T.ones[:], 1.0).then_inc(S.c1, 1)
+        g.wait_ge(S.c1, 1)
+        g.affine_select(T.selr[:], T.ones[:], [[0, 8], [1, 16]], A.is_equal, 0.0, 0, -1).then_inc(S.gl, 1)
+        g.affine_select(T.sels[:], T.ones[:], [[0, 8], [1, 16]], A.is_equal, 0.0, -1, -1).then_inc(S.gl, 1)
+        g.affine_select(T.selw[:], T.ones[:], [[0, 8], [1, 16]], A.is_equal, 0.0, 15, -1).then_inc(S.gl, 1)
+        v(V.memset(T.enf[:, 0:1], 0.0))
+    v(V.memset(T.nega[:], -9.0e29))
+    if rank is not None:
+        v(V.memset(T.zc[:, 16:32], 0.0))
+        v(V.memset(T.yc[:, 16:32], -7.0))
+        V.wait_ge(S.gi, 2)
+        v(V.tensor_scalar(T.dm[:], T.di[:], 15, None, A.bitwise_and))
+    vw()
+    v(V.tensor_scalar(T.negb[:], T.nega[:], 8.0, None, A.mult))
+    if rank is not None:
+        v(V.tensor_tensor(T.zc[:, 0:16], T.dm[:], T.dc[:], A.add))
+        v(V.tensor_tensor(T.yc[:, 0:16], T.dm[:], T.dc[:], A.add))
+        V.wait_ge(S.ldi, 32)
+        vw()
+        V.tensor_copy(T.enf[:, 1:17], T.en[:]).then_inc(S.vc, 1)
+        V.tensor_copy(T.idf[:], T.ix[:]).then_inc(S.vc, 1)
+        g.tensor.wait_ge(S.gl, 3)
+        g.tensor.wait_ge(S.vc, 2)
+        g.tensor.matmul(T.pse[:, 16:32], T.selr[:], T.enf[:, 1:17], True, True).then_inc(S.pe1, 1)
+        g.tensor.matmul(T.pse[:, 0:16], T.sels[:], T.enf[:, 1:17], True, False)
+        g.tensor.matmul(T.pse[:, 0:16], T.selw[:], T.enf[:, 0:16], False, True).then_inc(S.pe1, 1)
+        g.tensor.matmul(T.psi[:, 0:256], T.selr[:], T.idf[:], True, True).then_inc(S.pe2, 1)
+        V.wait_ge(S.pe1, 2)
+        v(V.tensor_copy(T.xx[:], T.pse[:, 0:32]))
+        vw()
+        v(V.tensor_tensor(T.ne[:, 0:16], T.xx[:, 16:32], T.xx[:, 0:16], A.is_gt))
+        v(V.tensor_tensor(T.ne[:, 16:32], T.xx[:, 16:32], T.xx[:, 0:16], A.is_gt))
+        v(V.tensor_tensor(T.w1[:], T.xx[:], T.yc[:], A.subtract))
+        vw()
+        v(V.tensor_tensor(T.w2[:], T.w1[:], T.ne[:], A.mult))
+        vw()
+        v(V.tensor_tensor(T.w3[:], T.w2[:], T.zc[:], A.add))
+        vw()
+        V.wait_ge(S.pe2, 1)
+        order = P["far"][rank] + P["peers"][rank] + [rank]
+        for q in order:
+            V.tensor_scalar(T.pk[:, q * PK:q * PK + 256], T.psi[:, 0:256], float(LO - R * q), float(LO + R),
+                            A.add, A.min).then_inc(S["k%d" % q], 1)
+            V.tensor_copy(T.pk[:, q * PK + 256:(q + 1) * PK], T.w3[:]).then_inc(S["k%d" % q], 1)
+        for rc, run in P["reqrelay"][rank]:
+            for q in run:
+                g.wait_ge(S["k%d" % q], 2)
+            send(rc, T.rb[:, 0:len(run) * PK], T.pk[:, run[0] * PK:(run[-1] + 1) * PK], "rl")
+        direct = P["peers"][rank]
+        if direct:
+            items = []
+            for q in direct:
+                g.wait_ge(S["k%d" % q], 2)
+                hc, j = P["at"][q, rank]
+                items.append(([hc], T["rq%d" % j][:], T.pk[:, q * PK:(q + 1) * PK], "rq%d" % j, P["rqmask"][q, rank]))
+            fused(items)
+        hc, j = P["at"][rank, rank]
+        if hc != core:
+            g.wait_ge(S["k%d" % rank], 2)
+            send(hc, T["rq%d" % j][:], T.pk[:, rank * PK:(rank + 1) * PK], "rq%d" % j)
+        for i, (a, b, h, k) in enumerate(ch):
+            if i == 0:
+                g.wait_ge(S.ldt0, 16)
+            if k == 2 and h == 0:
+                g.wait_ge(S.ldt1, 16)
+            send(helpers[h], T.tb[:, a:b], T.tb[:, a:b], "tco%d" % k)
+    else:
+        me = helpers.index(core)
+        others = [h for h in helpers if h != core]
+        for a, b, h, k in ch:
+            if h == me:
+                g.wait_ge(S["tco%d" % k], pop(topo.mask(cores[s], core)))
+                fused([(others, T.tb[:, a:b], T.tb[:, a:b], "tcf", topo.mask(core, others[0]))])
+
+    def table(q):
+        if rank is not None:
+            q.wait_ge(S.ldt0, 16)
+            q.wait_ge(S.ldt1, 16)
+        else:
+            for k in range(3):
+                q.wait_ge(S["tco%d" % k], pop(topo.mask(cores[s], core)))
+            q.wait_ge(S.tcf, 3 * sum(pop(topo.mask(h, core)) for h in helpers if h != core))
+
+    n = len(jobs)
+    x, (p1, p2) = MULTI if n > 1 else SINGLE
+    bounds = [(0, x), (x, x + p1), (x + p1, TT)]
+    V.tensor_copy(T.tb[:, 0:LO], T.negb[:, 0:LO]) if False else None
+    vw()
+    V.tensor_copy(T.tb[:, 0:LO], T.negb[:, 0:LO]).then_inc(S.sn, 1)
+    V.tensor_copy(T.tb[:, LO + R:W], T.negb[:, 0:8]).then_inc(S.sn, 1)
+    for j in range(n):
+        if jobs[j] == s:
+            v(V.memset(T["so%d" % j][:, 0:8], 0.0))
+        else:
+            v(V.tensor_copy(T["so%d" % j][:, 0:8], T.negb[:, 0:8]))
+        v(V.memset(T["mk%d" % j][:], 0.0))
+
+    def mask(j):
+        buf, o, sem, c = pkt(j)
+        V.wait_ge(sem, c)
+        vw()
+        v(V.tensor_copy(T["mk%d" % j][:, 0:TT + B].indirect(buf[:, o + 256:o + 272]), T.negb[:]))
+
+    def gather_v(j):
+        buf, o, sem, c = pkt(j)
+        v(V.tensor_copy(T["ga%d" % j][:, 0:x], T.tb[:, 0:W].indirect(buf[:, o:o + x // 16])))
+
+    def scans(j):
+        buf, o, sem, c = pkt(j)
+        so = T["so%d" % j]
+        for i, (a, b) in enumerate(bounds):
+            if i:
+                V.wait_ge(S["sa%d" % j] if i == 1 else S["sb%d" % j], 1)
+            vw()
+            init = 0.0 if i == 0 else so[:, 8 + a - 1:8 + a]
+            v(V.tensor_tensor_scan(so[:, 8 + a:8 + b], T["mk%d" % j][:, a:b], T["ga%d" % j][:, a:b], init, A.add, A.max))
+        vw()
+        mine = rank is not None and jobs[j] == rank
+        out = T["pt%d" % s] if mine else T["po%d" % j]
+        V.tensor_copy(out[:], so[:, 0:8 + TT].indirect(buf[:, o + 272:o + 288])).then_inc(S["pt%d" % s] if mine else S["ex%d" % j], 1)
+
+    table(SC)
+    SC.wait_ge(S.sn, 2)
+    for j in range(n):
+        buf, o, sem, c = pkt(j)
+        SC.wait_ge(sem, c)
+        for (a, b), nm in zip(bounds[1:], ("sa", "sb")):
+            SC.activation(T["ga%d" % j][:, a:b], T.tb[:, 0:W].indirect(buf[:, o + a // 16:o + b // 16]), F.Copy).then_inc(S[nm + str(j)], 1)
+    mask(0)
+    table(V)
+    V.wait_ge(S.sn, 2)
+    gather_v(0)
+    for j in range(n):
+        if j + 1 < n:
+            mask(j + 1)
+            gather_v(j + 1)
+        scans(j)
+    for j in range(n):
+        r = jobs[j]
+        if rank is not None and r == rank:
+            continue
+        g.wait_ge(S["ex%d" % j], 1)
+        if (s, r) in P["ret"] and rank is not None:
+            rc, i = P["ret"][s, r]
+            send(rc, T["rr%d" % i][:], T["po%d" % j][:], "rr%d" % i)
+        else:
+            send(cores[r], T["pt%d" % s][:], T["po%d" % j][:], "pt%d" % s)
+    if rank is not None:
+        def count(q):
+            hc, j = P["at"][q, rank]
+            if hc == core:
+                return 1
+            if (q, rank) in P["ret"] and hc == cores[q]:
+                return pop(topo.mask(P["ret"][q, rank][0], core))
+            return pop(topo.mask(hc, core))
+        early = [q for q in range(NR) if P["at"][q, rank][0] == cores[q]]
+        early = [q for q in early if q == rank] + [q for q in early if q != rank]
+        seq = early + [q for q in range(NR) if q not in early]
+        V.wait_ge(S["pt%d" % seq[0]], count(seq[0]))
+        for i in range(1, NR):
+            V.wait_ge(S["pt%d" % seq[i]], count(seq[i]))
+            vw()
+            in0 = T["pt%d" % seq[0]][:] if i == 1 else T.acc[:, 0:B]
+            if i < NR - 1:
+                v(V.tensor_tensor(T.acc[:, 0:B], in0, T["pt%d" % seq[i]][:], A.max))
+            else:
+                V.tensor_tensor(T.yb[:], in0, T["pt%d" % seq[i]][:], A.max).then_inc(S.yv, 1)
+        g.sync.wait_ge(S.yv, 1)
+        g.sync.dma_start(T.y[:], T.yb[:]).then_inc(S.yst, 16)
+        g.sync.wait_ge(S.yst, 16)
+    vw()
+    if cnt["loc"]:
+        g.wait_ge(S.loc, cnt["loc"])

@@ -7,9 +7,16 @@ PK = 256 + 32
 LO = 8
 W = LO + R + 8
 MAXJ = 3
-ROUNDS = (2560, 1792)
-MULTI = (1280, (1408, 1408))
-SINGLE = (1536, (1280, 1280))
+PIECES = [(0, 2560), (1, 2304), (2, 2048), (0, 1920), (1, 1920), (2, 2048), (1, 1280), (0, 1280), (3, 1024)]
+ALL = 3
+CUT = 6
+LATE = 8
+NVIA = 2
+CLEAR = 6
+SPLIT_OWN = (1408, 1792, 896)
+SPLIT_MULTI = (1088, 1664, 1344)
+SPLIT_LAST = (1344, 1728, 1024)
+SPLIT_SINGLE = (1408, 1664, 1024)
 
 SCRATCH = {
     "ix": ("sbuf", [16, 256], "int32"), "en": ("sbuf", [16, 16], "int32"),
@@ -21,7 +28,7 @@ SCRATCH = {
     "xx": ("sbuf", [128, 32], "float32"), "ne": ("sbuf", [128, 32], "float32"),
     "w1": ("sbuf", [128, 32], "float32"), "w2": ("sbuf", [128, 32], "float32"), "w3": ("sbuf", [128, 32], "float32"),
     "pk": ("sbuf", [128, NR * PK], "uint16"), "rb": ("sbuf", [128, NR * PK], "uint16"),
-    "nega": ("sbuf", [128, 256], "bfloat16"), "negb": ("sbuf", [128, 256], "bfloat16"),
+    "nega": ("sbuf", [128, 256], "bfloat16"), "negb": ("sbuf", [128, 256], "bfloat16"), "zs": ("sbuf", [128, 1024], "bfloat16"),
     "tb": ("sbuf", [128, W], "bfloat16"), "yb": ("sbuf", [128, B], "bfloat16"),
     "pse": ("psum", [128, 512], "float32"), "psi": ("psum", [128, 512], "float32"), "acc": ("psum", [128, 512], "float32"),
 }
@@ -34,8 +41,9 @@ for _j in range(MAXJ):
     SCRATCH["rr%d" % _j] = ("sbuf", [128, B], "bfloat16")
 for _r in range(NR):
     SCRATCH["pt%d" % _r] = ("sbuf", [128, B], "bfloat16")
-SEMAPHORES = (["ldi", "ldt0", "ldt1", "vv", "c1", "gl", "gi", "vc", "pe1", "pe2", "sn", "loc", "yv", "yst", "rl",
-               "tco0", "tco1", "tco2", "tcf"]
+SEMAPHORES = (["ldi", "ldt0", "ldt1", "vv", "c1", "gl", "gi", "vc", "pe1", "pe2", "sn", "zv", "zc", "loc", "yv", "yst", "rl",
+               "tcf", "tcd"]
+              + ["tco%d" % k for k in range(len(PIECES))]
               + ["k%d" % r for r in range(NR)] + ["pt%d" % r for r in range(NR)]
               + [n + str(j) for j in range(MAXJ) for n in ("rq", "rr", "ex", "sa", "sb")])
 
@@ -54,7 +62,8 @@ def split(mask, n):
 
 def plan(T, topo):
     every = range(topo.CORES_PER_CHIP * topo.CHIPS)
-    P = {"help": [], "relay": [], "jobs": {}, "at": {}, "ret": {}, "reqrelay": {}, "peers": [], "far": []}
+    P = {"help": [], "relay": [], "jobs": {}, "at": {}, "ret": {}, "reqrelay": {}, "peers": [], "far": [], "seq": [],
+         "soon": [], "later": [], "via": []}
     cores = [int(c) for c in T.cores]
     P["cores"] = cores
     for r in range(NR):
@@ -69,10 +78,16 @@ def plan(T, topo):
     for s in range(NR):
         h, peers, far = P["help"][s], P["peers"][s], P["far"][s]
         near = [p for p in peers if p > s] + [p for p in peers if p < s]
-        if len(far) <= 1:
+        first = h[0]
+        if len(far) <= 1 and len(P["via"]) < NVIA:
+            take = {cores[s]: [s] + near[0:1] + far, h[0]: near[1:2], h[1]: near[2:3], h[2]: near[3:4]}
+            P["via"].append(s)
+        elif len(far) <= 1:
             take = {cores[s]: [s] + near[0:2], h[0]: far, h[1]: near[2:3], h[2]: near[3:4]}
         else:
-            take = {cores[s]: far[2:], h[0]: far[0:1], h[1]: far[1:2], h[2]: [s]}
+            take = {cores[s]: [s] + far[2:4], h[0]: far[0:1], h[1]: far[1:2], h[2]: far[4:5]}
+            first = h[2]
+        P["seq"].append([first] + [c for c in h if c != first])
         for c in take:
             P["jobs"][c] = (s, take[c])
             for j, r in enumerate(take[c]):
@@ -84,36 +99,39 @@ def plan(T, topo):
                 runs[-1].append(s)
             else:
                 runs.append([s])
-        P["reqrelay"][r] = [(P["relay"][r][i % 2], run) for i, run in enumerate(runs)]
+        if len(runs) == 1:
+            P["reqrelay"][r] = [((P["relay"] if r in P["via"] else P["help"])[r][0], runs[0])]
+        else:
+            P["reqrelay"][r] = [(P["relay"][r][i % 2], run) for i, run in enumerate(runs)]
     for s in range(NR):
-        for i, r in enumerate([r for r in P["jobs"][cores[s]][1] if r != s and not topo.may_write(cores[s], cores[r])]):
-            P["ret"][s, r] = (P["relay"][s][i % 2], i // 2)
+        i = 0
+        for c in [cores[s]] + P["help"][s]:
+            for r in P["jobs"][c][1]:
+                if r != s and not topo.may_write(c, cores[r]):
+                    P["ret"][s, r] = (P["relay"][s][i % 2], i // 2)
+                    i += 1
     P["rqmask"] = {}
     for r in range(NR):
-        direct = [s for s in P["peers"][r]]
-        if direct:
-            ms = split(min(topo.mask(cores[r], P["at"][s, r][0]) for s in direct), len(direct))
-            for s, m in zip(direct, ms):
-                P["rqmask"][s, r] = m
+        P["soon"].append([s for s in P["peers"][r] if P["at"][s, r][0] == cores[s]])
+        P["later"].append([s for s in P["peers"][r] if P["at"][s, r][0] != cores[s]])
+        for part in (P["soon"][r], P["later"][r]):
+            if part:
+                ms = split(min(topo.mask(cores[r], P["at"][s, r][0]) for s in part), len(part))
+                for s, m in zip(part, ms):
+                    P["rqmask"][s, r] = m
         for rc, run in P["reqrelay"][r]:
             ms = split(topo.mask(rc, P["at"][run[0], r][0]), len(run))
             for s, m in zip(run, ms):
                 P["rqmask"][s, r] = m
-        if P["at"][r, r][0] != cores[r]:
-            P["rqmask"][r, r] = topo.mask(cores[r], P["at"][r, r][0])
     return P
 
 
 def chunks():
-    out, c = [], LO
-    left = R - 3 * sum(ROUNDS)
-    last = [left // 24 * 8] * 3
-    last[0] += left - sum(last)
-    for k in range(3):
-        for h in range(3):
-            w = ROUNDS[k] if k < 2 else last[h]
-            out.append((c, c + w, h, k))
-            c += w
+    out, c, n = [], LO, [0, 0, 0, 0]
+    for h, w in PIECES:
+        out.append((c, c + w, h, n[h]))
+        n[h] += 1
+        c += w
     return out
 
 
@@ -133,8 +151,8 @@ def rank_program(g, core, T, topo):
         if cnt["vv"]:
             V.wait_ge(S.vv, cnt["vv"])
 
-    def send(dst, out, in_, sem, m=None):
-        m = topo.mask(core, dst) if m is None else m
+    def send(dst, out, in_, sem):
+        m = topo.mask(core, dst)
         rid, pid, _ = topo.addr(dst)
         g.remote_dma(out, in_, S[sem], S.loc, pid, rid, m)
         cnt["loc"] += pop(m)
@@ -151,20 +169,29 @@ def rank_program(g, core, T, topo):
             cnt["loc"] += pop(m)
         g.remote_dma_fused(tr, local_sem=S.loc)
 
+    def lists(qs):
+        items = []
+        for q in qs:
+            g.wait_ge(S["k%d" % q], 2)
+            hc, j = P["at"][q, rank]
+            items.append(([hc], T["rq%d" % j][:], T.pk[:, q * PK:(q + 1) * PK], "rq%d" % j, P["rqmask"][q, rank]))
+        if items:
+            fused(items)
+
     for r in range(NR):
+        for rc, run in P["reqrelay"][r]:
+            if rc == core:
+                g.wait_ge(S.rl, pop(topo.mask(cores[r], core)))
+                items = []
+                for i, s in enumerate(run):
+                    hc, j = P["at"][s, r]
+                    items.append(([hc], T["rq%d" % j][:], T.rb[:, i * PK:(i + 1) * PK], "rq%d" % j, P["rqmask"][s, r]))
+                fused(items)
         if core in P["relay"][r]:
-            for rc, run in P["reqrelay"][r]:
-                if rc == core:
-                    g.wait_ge(S.rl, pop(topo.mask(cores[r], core)))
-                    items = []
-                    for i, s in enumerate(run):
-                        hc, j = P["at"][s, r]
-                        items.append(([hc], T["rq%d" % j][:], T.rb[:, i * PK:(i + 1) * PK], "rq%d" % j, P["rqmask"][s, r]))
-                    fused(items)
-            for q in P["jobs"][cores[r]][1]:
+            for q in [q for c in [cores[r]] + P["help"][r] for q in P["jobs"][c][1]]:
                 if P["ret"].get((r, q), (None, 0))[0] == core:
                     i = P["ret"][r, q][1]
-                    g.wait_ge(S["rr%d" % i], pop(topo.mask(cores[r], core)))
+                    g.wait_ge(S["rr%d" % i], pop(topo.mask(P["at"][r, q][0], core)))
                     send(cores[q], T["pt%d" % r][:], T["rr%d" % i][:], "pt%d" % r)
     if core not in P["jobs"]:
         if cnt["loc"]:
@@ -172,19 +199,20 @@ def rank_program(g, core, T, topo):
         return
 
     s, jobs = P["jobs"][core]
+    n = len(jobs)
     ch = chunks()
-    helpers = P["help"][s]
+    helpers = P["seq"][s]
 
     def pkt(j):
         r = jobs[j]
-        if rank is not None and r == rank:
+        if r == s:
             return T.pk, rank * PK, S["k%d" % rank], 2
         return T["rq%d" % j], 0, S["rq%d" % j], pop(P["rqmask"][s, r])
 
     if rank is not None:
         g.sync.dma_start(T.ix[:], T.idx[:]).then_inc(S.ldi, 16)
         SC.dma_start(T.en[:], T.end[:]).then_inc(S.ldi, 16)
-        cut = ch[6][0]
+        cut = ch[CUT][0]
         g.sync.dma_start(T.tb[:, LO:cut], T.tab[:, 0:cut - LO]).then_inc(S.ldt0, 16)
         g.sync.dma_start(T.tb[:, cut:LO + R], T.tab[:, cut - LO:R]).then_inc(S.ldt1, 16)
         g.iota(T.di[:], [[0, 16]], 0, 1).then_inc(S.gi, 1)
@@ -195,6 +223,11 @@ def rank_program(g, core, T, topo):
         g.affine_select(T.sels[:], T.ones[:], [[0, 8], [1, 16]], A.is_equal, 0.0, -1, -1).then_inc(S.gl, 1)
         g.affine_select(T.selw[:], T.ones[:], [[0, 8], [1, 16]], A.is_equal, 0.0, 15, -1).then_inc(S.gl, 1)
         v(V.memset(T.enf[:, 0:1], 0.0))
+    V.memset(T.zs[:], 0.0).then_inc(S.zv, 1)
+    SC.wait_ge(S.zv, 1)
+    nc = min(CLEAR, 4 * n)
+    for q in range(nc):
+        SC.activation(T["mk%d" % (q // 4)][:, q % 4 * 1024:(q % 4 + 1) * 1024], T.zs[:], F.Copy).then_inc(S.zc, 1)
     v(V.memset(T.nega[:], -9.0e29))
     if rank is not None:
         v(V.memset(T.zc[:, 16:32], 0.0))
@@ -228,8 +261,7 @@ def rank_program(g, core, T, topo):
         v(V.tensor_tensor(T.w3[:], T.w2[:], T.zc[:], A.add))
         vw()
         V.wait_ge(S.pe2, 1)
-        order = P["far"][rank] + P["peers"][rank] + [rank]
-        for q in order:
+        for q in P["far"][rank] + P["soon"][rank] + [rank] + P["later"][rank]:
             V.tensor_scalar(T.pk[:, q * PK:q * PK + 256], T.psi[:, 0:256], float(LO - R * q), float(LO + R),
                             A.add, A.min).then_inc(S["k%d" % q], 1)
             V.tensor_copy(T.pk[:, q * PK + 256:(q + 1) * PK], T.w3[:]).then_inc(S["k%d" % q], 1)
@@ -237,24 +269,18 @@ def rank_program(g, core, T, topo):
             for q in run:
                 g.wait_ge(S["k%d" % q], 2)
             send(rc, T.rb[:, 0:len(run) * PK], T.pk[:, run[0] * PK:(run[-1] + 1) * PK], "rl")
-        direct = P["peers"][rank]
-        if direct:
-            items = []
-            for q in direct:
-                g.wait_ge(S["k%d" % q], 2)
-                hc, j = P["at"][q, rank]
-                items.append(([hc], T["rq%d" % j][:], T.pk[:, q * PK:(q + 1) * PK], "rq%d" % j, P["rqmask"][q, rank]))
-            fused(items)
-        hc, j = P["at"][rank, rank]
-        if hc != core:
-            g.wait_ge(S["k%d" % rank], 2)
-            send(hc, T["rq%d" % j][:], T.pk[:, rank * PK:(rank + 1) * PK], "rq%d" % j)
+        lists(P["soon"][rank])
         for i, (a, b, h, k) in enumerate(ch):
             if i == 0:
                 g.wait_ge(S.ldt0, 16)
-            if k == 2 and h == 0:
+            if i == CUT:
                 g.wait_ge(S.ldt1, 16)
-            send(helpers[h], T.tb[:, a:b], T.tb[:, a:b], "tco%d" % k)
+            if i == LATE:
+                lists(P["later"][rank])
+            if h == ALL:
+                fused([(helpers, T.tb[:, a:b], T.tb[:, a:b], "tcd", topo.mask(core, helpers[0]))])
+            else:
+                send(helpers[h], T.tb[:, a:b], T.tb[:, a:b], "tco%d" % k)
     else:
         me = helpers.index(core)
         others = [h for h in helpers if h != core]
@@ -268,14 +294,29 @@ def rank_program(g, core, T, topo):
             q.wait_ge(S.ldt0, 16)
             q.wait_ge(S.ldt1, 16)
         else:
-            for k in range(3):
-                q.wait_ge(S["tco%d" % k], pop(topo.mask(cores[s], core)))
-            q.wait_ge(S.tcf, 3 * sum(pop(topo.mask(h, core)) for h in helpers if h != core))
+            for a, b, h, k in ch:
+                if h == me:
+                    q.wait_ge(S["tco%d" % k], pop(topo.mask(cores[s], core)))
+            q.wait_ge(S.tcd, pop(topo.mask(cores[s], core)))
+            q.wait_ge(S.tcf, sum(pop(topo.mask(helpers[h], core)) for a, b, h, k in ch if h not in (me, ALL)))
 
-    n = len(jobs)
-    x, (p1, p2) = MULTI if n > 1 else SINGLE
-    bounds = [(0, x), (x, x + p1), (x + p1, TT)]
-    V.tensor_copy(T.tb[:, 0:LO], T.negb[:, 0:LO]) if False else None
+    if n == 1:
+        cuts = [SPLIT_SINGLE]
+        sc_seq = [(0, 1), (0, 2)]
+        v_seq = ["m0", "T", "g0", "s00", "s01", "s02", "e0"]
+        out_seq = [0]
+    elif P["peers"][s]:
+        cuts = [SPLIT_OWN, SPLIT_MULTI, SPLIT_MULTI]
+        sc_seq = [(0, 1), (1, 1), (1, 2), (2, 1), (2, 2), (0, 2)]
+        v_seq = ["m0", "T", "g0", "m1", "g1", "s00", "s01", "m2", "g2", "s10", "s11", "s12", "e1", "s20", "s21", "s22", "e2", "s02", "e0"]
+        out_seq = [1, 2]
+    else:
+        cuts = [SPLIT_MULTI, SPLIT_MULTI, SPLIT_LAST]
+        sc_seq = [(0, 1), (0, 2), (1, 1), (1, 2), (2, 1), (2, 2)]
+        v_seq = ["m0", "T", "g0", "s00", "s01", "s02", "e0", "m1", "g1", "m2", "g2", "s10", "s11", "s12", "e1", "s20", "s21", "s22", "e2"]
+        out_seq = [1, 2]
+    bounds = [[(0, x), (x, x + p), (x + p, x + p + q)] for x, p, q in cuts]
+
     vw()
     V.tensor_copy(T.tb[:, 0:LO], T.negb[:, 0:LO]).then_inc(S.sn, 1)
     V.tensor_copy(T.tb[:, LO + R:W], T.negb[:, 0:8]).then_inc(S.sn, 1)
@@ -284,54 +325,52 @@ def rank_program(g, core, T, topo):
             v(V.memset(T["so%d" % j][:, 0:8], 0.0))
         else:
             v(V.tensor_copy(T["so%d" % j][:, 0:8], T.negb[:, 0:8]))
-        v(V.memset(T["mk%d" % j][:], 0.0))
+        lo = min(4, max(0, nc - 4 * j)) * 1024
+        if lo < TT:
+            v(V.memset(T["mk%d" % j][:, lo:TT], 0.0))
+    V.wait_ge(S.zc, nc)
 
-    def mask(j):
+    for op in v_seq:
+        if op == "T":
+            table(V)
+            V.wait_ge(S.sn, 2)
+            continue
+        j = int(op[1])
         buf, o, sem, c = pkt(j)
-        V.wait_ge(sem, c)
-        vw()
-        v(V.tensor_copy(T["mk%d" % j][:, 0:TT + B].indirect(buf[:, o + 256:o + 272]), T.negb[:]))
-
-    def gather_v(j):
-        buf, o, sem, c = pkt(j)
-        v(V.tensor_copy(T["ga%d" % j][:, 0:x], T.tb[:, 0:W].indirect(buf[:, o:o + x // 16])))
-
-    def scans(j):
-        buf, o, sem, c = pkt(j)
-        so = T["so%d" % j]
-        for i, (a, b) in enumerate(bounds):
+        so, ga, mk = T["so%d" % j], T["ga%d" % j], T["mk%d" % j]
+        if op[0] == "m":
+            V.wait_ge(sem, c)
+            vw()
+            v(V.tensor_copy(mk[:, 0:TT + B].indirect(buf[:, o + 256:o + 272]), T.negb[:]))
+        elif op[0] == "g":
+            x = cuts[j][0]
+            v(V.tensor_copy(ga[:, 0:x], T.tb[:, 0:W].indirect(buf[:, o:o + x // 16])))
+        elif op[0] == "s":
+            i = int(op[2])
+            a, b = bounds[j][i]
             if i:
-                V.wait_ge(S["sa%d" % j] if i == 1 else S["sb%d" % j], 1)
+                V.wait_ge(S["s" + "ab"[i - 1] + str(j)], 1)
             vw()
             init = 0.0 if i == 0 else so[:, 8 + a - 1:8 + a]
-            v(V.tensor_tensor_scan(so[:, 8 + a:8 + b], T["mk%d" % j][:, a:b], T["ga%d" % j][:, a:b], init, A.add, A.max))
-        vw()
-        mine = rank is not None and jobs[j] == rank
-        out = T["pt%d" % s] if mine else T["po%d" % j]
-        V.tensor_copy(out[:], so[:, 0:8 + TT].indirect(buf[:, o + 272:o + 288])).then_inc(S["pt%d" % s] if mine else S["ex%d" % j], 1)
+            v(V.tensor_tensor_scan(so[:, 8 + a:8 + b], mk[:, a:b], ga[:, a:b], init, A.add, A.max))
+        else:
+            vw()
+            out, done = (T["pt%d" % s], S["pt%d" % s]) if jobs[j] == s else (T["po%d" % j], S["ex%d" % j])
+            V.tensor_copy(out[:], so[:, 0:8 + TT].indirect(buf[:, o + 272:o + 288])).then_inc(done, 1)
 
     table(SC)
     SC.wait_ge(S.sn, 2)
-    for j in range(n):
+    for j, i in sc_seq:
         buf, o, sem, c = pkt(j)
-        SC.wait_ge(sem, c)
-        for (a, b), nm in zip(bounds[1:], ("sa", "sb")):
-            SC.activation(T["ga%d" % j][:, a:b], T.tb[:, 0:W].indirect(buf[:, o + a // 16:o + b // 16]), F.Copy).then_inc(S[nm + str(j)], 1)
-    mask(0)
-    table(V)
-    V.wait_ge(S.sn, 2)
-    gather_v(0)
-    for j in range(n):
-        if j + 1 < n:
-            mask(j + 1)
-            gather_v(j + 1)
-        scans(j)
-    for j in range(n):
+        if i == 1:
+            SC.wait_ge(sem, c)
+        a, b = bounds[j][i]
+        SC.activation(T["ga%d" % j][:, a:b], T.tb[:, 0:W].indirect(buf[:, o + a // 16:o + b // 16]),
+                      F.Copy).then_inc(S["s" + "ab"[i - 1] + str(j)], 1)
+    for j in out_seq:
         r = jobs[j]
-        if rank is not None and r == rank:
-            continue
         g.wait_ge(S["ex%d" % j], 1)
-        if (s, r) in P["ret"] and rank is not None:
+        if (s, r) in P["ret"]:
             rc, i = P["ret"][s, r]
             send(rc, T["rr%d" % i][:], T["po%d" % j][:], "rr%d" % i)
         else:
@@ -341,12 +380,14 @@ def rank_program(g, core, T, topo):
             hc, j = P["at"][q, rank]
             if hc == core:
                 return 1
-            if (q, rank) in P["ret"] and hc == cores[q]:
-                return pop(topo.mask(P["ret"][q, rank][0], core))
-            return pop(topo.mask(hc, core))
-        early = [q for q in range(NR) if P["at"][q, rank][0] == cores[q]]
-        early = [q for q in early if q == rank] + [q for q in early if q != rank]
-        seq = early + [q for q in range(NR) if q not in early]
+            return pop(topo.mask(P["ret"][q, rank][0] if (q, rank) in P["ret"] else hc, core))
+
+        def when(q):
+            if q == rank:
+                return 0
+            early = P["at"][q, rank][0] == cores[q]
+            return (2.5 if early else 3) if q in P["far"][rank] else 1 if early else 2
+        seq = sorted(range(NR), key=when)
         V.wait_ge(S["pt%d" % seq[0]], count(seq[0]))
         for i in range(1, NR):
             V.wait_ge(S["pt%d" % seq[i]], count(seq[i]))

import numpy as np
from concourse.bass import DstId, RemoteDMATransfer
from concourse.mybir import AluOpType as A, ActivationFunctionType as F

NR, R, TT, B = 6, 16384, 4096, 256
PK = 256 + 32
LO = 8
W = LO + R + 8
MAXJ = 3
PIECES = [(0, 2560), (1, 2304), (2, 2048), (0, 1920), (1, 1920), (2, 2048), (1, 1280), (0, 1280), (3, 1024)]
ALL = 3
CUT = 6
LATE = 8
NVIA = 2
CLEAR = 6
SPLIT_OWN = (1408, 1792, 896)
SPLIT_MULTI = (1088, 1664, 1344)
SPLIT_LAST = (1344, 1728, 1024)
SPLIT_SINGLE = (1408, 1664, 1024)

SCRATCH = {
    "ix": ("sbuf", [16, 256], "int32"), "en": ("sbuf", [16, 16], "int32"),
    "idf": ("sbuf", [16, 256], "float32"), "enf": ("sbuf", [16, 32], "float32"),
    "ones": ("sbuf", [16, 128], "float32"),
    "selr": ("sbuf", [16, 128], "float32"), "sels": ("sbuf", [16, 128], "float32"), "selw": ("sbuf", [16, 128], "float32"),
    "di": ("sbuf", [128, 16], "int32"), "dm": ("sbuf", [128, 16], "int32"), "dc": ("sbuf", [128, 16], "int32"),
    "zc": ("sbuf", [128, 32], "float32"), "yc": ("sbuf", [128, 32], "float32"),
    "xx": ("sbuf", [128, 32], "float32"), "ne": ("sbuf", [128, 32], "float32"),
    "w1": ("sbuf", [128, 32], "float32"), "w2": ("sbuf", [128, 32], "float32"), "w3": ("sbuf", [128, 32], "float32"),
    "pk": ("sbuf", [128, NR * PK], "uint16"), "rb": ("sbuf", [128, NR * PK], "uint16"),
    "nega": ("sbuf", [128, 256], "bfloat16"), "negb": ("sbuf", [128, 256], "bfloat16"), "zs": ("sbuf", [128, 1024], "bfloat16"),
    "tb": ("sbuf", [128, W], "bfloat16"), "yb": ("sbuf", [128, B], "bfloat16"),
    "pse": ("psum", [128, 512], "float32"), "psi": ("psum", [128, 512], "float32"), "acc": ("psum", [128, 512], "float32"),
}
for _j in range(MAXJ):
    SCRATCH["rq%d" % _j] = ("sbuf", [128, PK], "uint16")
    SCRATCH["mk%d" % _j] = ("sbuf", [128, TT + B], "bfloat16")
    SCRATCH["ga%d" % _j] = ("sbuf", [128, TT], "bfloat16")
    SCRATCH["so%d" % _j] = ("sbuf", [128, 8 + TT], "bfloat16")
    SCRATCH["po%d" % _j] = ("sbuf", [128, B], "bfloat16")
    SCRATCH["rr%d" % _j] = ("sbuf", [128, B], "bfloat16")
for _r in range(NR):
    SCRATCH["pt%d" % _r] = ("sbuf", [128, B], "bfloat16")
SEMAPHORES = (["ldi", "ldt0", "ldt1", "vv", "c1", "gl", "gi", "vc", "pe1", "pe2", "sn", "zv", "zc", "loc", "yv", "yst", "rl",
               "tcf", "tcd"]
              + ["tco%d" % k for k in range(len(PIECES))]
              + ["k%d" % r for r in range(NR)] + ["pt%d" % r for r in range(NR)]
              + [n + str(j) for j in range(MAXJ) for n in ("rq", "rr", "ex", "sa", "sb")])


def pop(m):
    return bin(m).count("1")


def split(mask, n):
    bits = [b for b in range(32) if mask >> b & 1]
    k = 1
    while 2 * k * n <= len(bits):
        k *= 2
    return [sum(1 << b for b in bits[i * k:(i + 1) * k]) for i in range(n)]


def plan(T, topo):
    every = range(topo.CORES_PER_CHIP * topo.CHIPS)
    P = {"help": [], "relay": [], "jobs": {}, "at": {}, "ret": {}, "reqrelay": {}, "peers": [], "far": [], "seq": [],
         "soon": [], "later": [], "via": []}
    cores = [int(c) for c in T.cores]
    P["cores"] = cores
    for r in range(NR):
        own = [c for c in every if topo.chip(c) == topo.chip(cores[r])]
        other = [c for c in every if topo.mates(topo.chip(c), topo.chip(cores[r]))][0]
        port = [c for c in own if topo.may_write(c, other)]
        mine = [c for c in own if topo.die(c) == topo.die(cores[r]) and c != cores[r]]
        P["help"].append([c for c in mine if c in port] + [c for c in mine if c not in port])
        P["relay"].append([c for c in port if topo.die(c) != topo.die(cores[r])])
        P["peers"].append([s for s in range(NR) if s != r and topo.may_write(cores[r], cores[s])])
        P["far"].append([s for s in range(NR) if s != r and not topo.may_write(cores[r], cores[s])])
    for s in range(NR):
        h, peers, far = P["help"][s], P["peers"][s], P["far"][s]
        near = [p for p in peers if p > s] + [p for p in peers if p < s]
        first = h[0]
        if len(far) <= 1 and len(P["via"]) < NVIA:
            take = {cores[s]: [s] + near[0:1] + far, h[0]: near[1:2], h[1]: near[2:3], h[2]: near[3:4]}
            P["via"].append(s)
        elif len(far) <= 1:
            take = {cores[s]: [s] + near[0:2], h[0]: far, h[1]: near[2:3], h[2]: near[3:4]}
        else:
            take = {cores[s]: [s] + far[2:4], h[0]: far[0:1], h[1]: far[1:2], h[2]: far[4:5]}
            first = h[2]
        P["seq"].append([first] + [c for c in h if c != first])
        for c in take:
            P["jobs"][c] = (s, take[c])
            for j, r in enumerate(take[c]):
                P["at"][s, r] = (c, j)
    for r in range(NR):
        runs = []
        for s in P["far"][r]:
            if runs and runs[-1][-1] == s - 1:
                runs[-1].append(s)
            else:
                runs.append([s])
        if len(runs) == 1:
            P["reqrelay"][r] = [((P["relay"] if r in P["via"] else P["help"])[r][0], runs[0])]
        else:
            P["reqrelay"][r] = [(P["relay"][r][i % 2], run) for i, run in enumerate(runs)]
    for s in range(NR):
        i = 0
        for c in [cores[s]] + P["help"][s]:
            for r in P["jobs"][c][1]:
                if r != s and not topo.may_write(c, cores[r]):
                    P["ret"][s, r] = (P["relay"][s][i % 2], i // 2)
                    i += 1
    P["rqmask"] = {}
    for r in range(NR):
        P["soon"].append([s for s in P["peers"][r] if P["at"][s, r][0] == cores[s]])
        P["later"].append([s for s in P["peers"][r] if P["at"][s, r][0] != cores[s]])
        for part in (P["soon"][r], P["later"][r]):
            if part:
                ms = split(min(topo.mask(cores[r], P["at"][s, r][0]) for s in part), len(part))
                for s, m in zip(part, ms):
                    P["rqmask"][s, r] = m
        for rc, run in P["reqrelay"][r]:
            ms = split(topo.mask(rc, P["at"][run[0], r][0]), len(run))
            for s, m in zip(run, ms):
                P["rqmask"][s, r] = m
    return P


def chunks():
    out, c, n = [], LO, [0, 0, 0, 0]
    for h, w in PIECES:
        out.append((c, c + w, h, n[h]))
        n[h] += 1
        c += w
    return out


def rank_program(g, core, T, topo):
    P = plan(T, topo)
    cores = P["cores"]
    rank = T.rank_of(core)
    S = T.sem
    cnt = {"vv": 0, "loc": 0}
    V, SC = g.vector, g.scalar

    def v(ins):
        ins.then_inc(S.vv, 1)
        cnt["vv"] += 1

    def vw():
        if cnt["vv"]:
            V.wait_ge(S.vv, cnt["vv"])

    def send(dst, out, in_, sem):
        m = topo.mask(core, dst)
        rid, pid, _ = topo.addr(dst)
        g.remote_dma(out, in_, S[sem], S.loc, pid, rid, m)
        cnt["loc"] += pop(m)

    def fused(items):
        tr = []
        for dsts, out, in_, sem, m in items:
            ids = []
            for d in dsts:
                rid, pid, _ = topo.addr(d)
                ids.append(DstId(rid=rid, pnc=pid))
            tr.append(RemoteDMATransfer(dst_ids=ids, dma_engine_mask=m, remote_sem=S[sem], srcs=[in_],
                                        dsts=[out for _ in dsts], alu_op=0))
            cnt["loc"] += pop(m)
        g.remote_dma_fused(tr, local_sem=S.loc)

    def lists(qs):
        items = []
        for q in qs:
            g.wait_ge(S["k%d" % q], 2)
            hc, j = P["at"][q, rank]
            items.append(([hc], T["rq%d" % j][:], T.pk[:, q * PK:(q + 1) * PK], "rq%d" % j, P["rqmask"][q, rank]))
        if items:
            fused(items)

    for r in range(NR):
        for rc, run in P["reqrelay"][r]:
            if rc == core:
                g.wait_ge(S.rl, pop(topo.mask(cores[r], core)))
                items = []
                for i, s in enumerate(run):
                    hc, j = P["at"][s, r]
                    items.append(([hc], T["rq%d" % j][:], T.rb[:, i * PK:(i + 1) * PK], "rq%d" % j, P["rqmask"][s, r]))
                fused(items)
        if core in P["relay"][r]:
            for q in [q for c in [cores[r]] + P["help"][r] for q in P["jobs"][c][1]]:
                if P["ret"].get((r, q), (None, 0))[0] == core:
                    i = P["ret"][r, q][1]
                    g.wait_ge(S["rr%d" % i], pop(topo.mask(P["at"][r, q][0], core)))
                    send(cores[q], T["pt%d" % r][:], T["rr%d" % i][:], "pt%d" % r)
    if core not in P["jobs"]:
        if cnt["loc"]:
            g.wait_ge(S.loc, cnt["loc"])
        return

    s, jobs = P["jobs"][core]
    n = len(jobs)
    ch = chunks()
    helpers = P["seq"][s]

    def pkt(j):
        r = jobs[j]
        if r == s:
            return T.pk, rank * PK, S["k%d" % rank], 2
        return T["rq%d" % j], 0, S["rq%d" % j], pop(P["rqmask"][s, r])

    if rank is not None:
        g.sync.dma_start(T.ix[:], T.idx[:]).then_inc(S.ldi, 16)
        SC.dma_start(T.en[:], T.end[:]).then_inc(S.ldi, 16)
        cut = ch[CUT][0]
        g.sync.dma_start(T.tb[:, LO:cut], T.tab[:, 0:cut - LO]).then_inc(S.ldt0, 16)
        g.sync.dma_start(T.tb[:, cut:LO + R], T.tab[:, cut - LO:R]).then_inc(S.ldt1, 16)
        g.iota(T.di[:], [[0, 16]], 0, 1).then_inc(S.gi, 1)
        g.iota(T.dc[:], [[16, 16]], TT, 0).then_inc(S.gi, 1)
        V.memset(T.ones[:], 1.0).then_inc(S.c1, 1)
        g.wait_ge(S.c1, 1)
        g.affine_select(T.selr[:], T.ones[:], [[0, 8], [1, 16]], A.is_equal, 0.0, 0, -1).then_inc(S.gl, 1)
        g.affine_select(T.sels[:], T.ones[:], [[0, 8], [1, 16]], A.is_equal, 0.0, -1, -1).then_inc(S.gl, 1)
        g.affine_select(T.selw[:], T.ones[:], [[0, 8], [1, 16]], A.is_equal, 0.0, 15, -1).then_inc(S.gl, 1)
        v(V.memset(T.enf[:, 0:1], 0.0))
    V.memset(T.zs[:], 0.0).then_inc(S.zv, 1)
    SC.wait_ge(S.zv, 1)
    nc = min(CLEAR, 4 * n)
    for q in range(nc):
        SC.activation(T["mk%d" % (q // 4)][:, q % 4 * 1024:(q % 4 + 1) * 1024], T.zs[:], F.Copy).then_inc(S.zc, 1)
    v(V.memset(T.nega[:], -9.0e29))
    if rank is not None:
        v(V.memset(T.zc[:, 16:32], 0.0))
        v(V.memset(T.yc[:, 16:32], -7.0))
        V.wait_ge(S.gi, 2)
        v(V.tensor_scalar(T.dm[:], T.di[:], 15, None, A.bitwise_and))
    vw()
    v(V.tensor_scalar(T.negb[:], T.nega[:], 8.0, None, A.mult))
    if rank is not None:
        v(V.tensor_tensor(T.zc[:, 0:16], T.dm[:], T.dc[:], A.add))
        v(V.tensor_tensor(T.yc[:, 0:16], T.dm[:], T.dc[:], A.add))
        V.wait_ge(S.ldi, 32)
        vw()
        V.tensor_copy(T.enf[:, 1:17], T.en[:]).then_inc(S.vc, 1)
        V.tensor_copy(T.idf[:], T.ix[:]).then_inc(S.vc, 1)
        g.tensor.wait_ge(S.gl, 3)
        g.tensor.wait_ge(S.vc, 2)
        g.tensor.matmul(T.pse[:, 16:32], T.selr[:], T.enf[:, 1:17], True, True).then_inc(S.pe1, 1)
        g.tensor.matmul(T.pse[:, 0:16], T.sels[:], T.enf[:, 1:17], True, False)
        g.tensor.matmul(T.pse[:, 0:16], T.selw[:], T.enf[:, 0:16], False, True).then_inc(S.pe1, 1)
        g.tensor.matmul(T.psi[:, 0:256], T.selr[:], T.idf[:], True, True).then_inc(S.pe2, 1)
        V.wait_ge(S.pe1, 2)
        v(V.tensor_copy(T.xx[:], T.pse[:, 0:32]))
        vw()
        v(V.tensor_tensor(T.ne[:, 0:16], T.xx[:, 16:32], T.xx[:, 0:16], A.is_gt))
        v(V.tensor_tensor(T.ne[:, 16:32], T.xx[:, 16:32], T.xx[:, 0:16], A.is_gt))
        v(V.tensor_tensor(T.w1[:], T.xx[:], T.yc[:], A.subtract))
        vw()
        v(V.tensor_tensor(T.w2[:], T.w1[:], T.ne[:], A.mult))
        vw()
        v(V.tensor_tensor(T.w3[:], T.w2[:], T.zc[:], A.add))
        vw()
        V.wait_ge(S.pe2, 1)
        for q in P["far"][rank] + P["soon"][rank] + [rank] + P["later"][rank]:
            V.tensor_scalar(T.pk[:, q * PK:q * PK + 256], T.psi[:, 0:256], float(LO - R * q), float(LO + R),
                            A.add, A.min).then_inc(S["k%d" % q], 1)
            V.tensor_copy(T.pk[:, q * PK + 256:(q + 1) * PK], T.w3[:]).then_inc(S["k%d" % q], 1)
        for rc, run in P["reqrelay"][rank]:
            for q in run:
                g.wait_ge(S["k%d" % q], 2)
            send(rc, T.rb[:, 0:len(run) * PK], T.pk[:, run[0] * PK:(run[-1] + 1) * PK], "rl")
        lists(P["soon"][rank])
        for i, (a, b, h, k) in enumerate(ch):
            if i == 0:
                g.wait_ge(S.ldt0, 16)
            if i == CUT:
                g.wait_ge(S.ldt1, 16)
            if i == LATE:
                lists(P["later"][rank])
            if h == ALL:
                fused([(helpers, T.tb[:, a:b], T.tb[:, a:b], "tcd", topo.mask(core, helpers[0]))])
            else:
                send(helpers[h], T.tb[:, a:b], T.tb[:, a:b], "tco%d" % k)
    else:
        me = helpers.index(core)
        others = [h for h in helpers if h != core]
        for a, b, h, k in ch:
            if h == me:
                g.wait_ge(S["tco%d" % k], pop(topo.mask(cores[s], core)))
                fused([(others, T.tb[:, a:b], T.tb[:, a:b], "tcf", topo.mask(core, others[0]))])

    def table(q):
        if rank is not None:
            q.wait_ge(S.ldt0, 16)
            q.wait_ge(S.ldt1, 16)
        else:
            for a, b, h, k in ch:
                if h == me:
                    q.wait_ge(S["tco%d" % k], pop(topo.mask(cores[s], core)))
            q.wait_ge(S.tcd, pop(topo.mask(cores[s], core)))
            q.wait_ge(S.tcf, sum(pop(topo.mask(helpers[h], core)) for a, b, h, k in ch if h not in (me, ALL)))

    if n == 1:
        cuts = [SPLIT_SINGLE]
        sc_seq = [(0, 1), (0, 2)]
        v_seq = ["m0", "T", "g0", "s00", "s01", "s02", "e0"]
        out_seq = [0]
    elif P["peers"][s]:
        cuts = [SPLIT_OWN, SPLIT_MULTI, SPLIT_MULTI]
        sc_seq = [(0, 1), (1, 1), (1, 2), (2, 1), (2, 2), (0, 2)]
        v_seq = ["m0", "T", "g0", "m1", "g1", "s00", "s01", "m2", "g2", "s10", "s11", "s12", "e1", "s20", "s21", "s22", "e2", "s02", "e0"]
        out_seq = [1, 2]
    else:
        cuts = [SPLIT_MULTI, SPLIT_MULTI, SPLIT_LAST]
        sc_seq = [(0, 1), (0, 2), (1, 1), (1, 2), (2, 1), (2, 2)]
        v_seq = ["m0", "T", "g0", "s00", "s01", "s02", "e0", "m1", "g1", "m2", "g2", "s10", "s11", "s12", "e1", "s20", "s21", "s22", "e2"]
        out_seq = [1, 2]
    bounds = [[(0, x), (x, x + p), (x + p, x + p + q)] for x, p, q in cuts]

    vw()
    V.tensor_copy(T.tb[:, 0:LO], T.negb[:, 0:LO]).then_inc(S.sn, 1)
    V.tensor_copy(T.tb[:, LO + R:W], T.negb[:, 0:8]).then_inc(S.sn, 1)
    for j in range(n):
        if jobs[j] == s:
            v(V.memset(T["so%d" % j][:, 0:8], 0.0))
        else:
            v(V.tensor_copy(T["so%d" % j][:, 0:8], T.negb[:, 0:8]))
        lo = min(4, max(0, nc - 4 * j)) * 1024
        if lo < TT:
            v(V.memset(T["mk%d" % j][:, lo:TT], 0.0))
    V.wait_ge(S.zc, nc)

    for op in v_seq:
        if op == "T":
            table(V)
            V.wait_ge(S.sn, 2)
            continue
        j = int(op[1])
        buf, o, sem, c = pkt(j)
        so, ga, mk = T["so%d" % j], T["ga%d" % j], T["mk%d" % j]
        if op[0] == "m":
            V.wait_ge(sem, c)
            vw()
            v(V.tensor_copy(mk[:, 0:TT + B].indirect(buf[:, o + 256:o + 272]), T.negb[:]))
        elif op[0] == "g":
            x = cuts[j][0]
            v(V.tensor_copy(ga[:, 0:x], T.tb[:, 0:W].indirect(buf[:, o:o + x // 16])))
        elif op[0] == "s":
            i = int(op[2])
            a, b = bounds[j][i]
            if i:
                V.wait_ge(S["s" + "ab"[i - 1] + str(j)], 1)
            vw()
            init = 0.0 if i == 0 else so[:, 8 + a - 1:8 + a]
            v(V.tensor_tensor_scan(so[:, 8 + a:8 + b], mk[:, a:b], ga[:, a:b], init, A.add, A.max))
        else:
            vw()
            out, done = (T["pt%d" % s], S["pt%d" % s]) if jobs[j] == s else (T["po%d" % j], S["ex%d" % j])
            V.tensor_copy(out[:], so[:, 0:8 + TT].indirect(buf[:, o + 272:o + 288])).then_inc(done, 1)

    table(SC)
    SC.wait_ge(S.sn, 2)
    for j, i in sc_seq:
        buf, o, sem, c = pkt(j)
        if i == 1:
            SC.wait_ge(sem, c)
        a, b = bounds[j][i]
        SC.activation(T["ga%d" % j][:, a:b], T.tb[:, 0:W].indirect(buf[:, o + a // 16:o + b // 16]),
                      F.Copy).then_inc(S["s" + "ab"[i - 1] + str(j)], 1)
    for j in out_seq:
        r = jobs[j]
        g.wait_ge(S["ex%d" % j], 1)
        if (s, r) in P["ret"]:
            rc, i = P["ret"][s, r]
            send(rc, T["rr%d" % i][:], T["po%d" % j][:], "rr%d" % i)
        else:
            send(cores[r], T["pt%d" % s][:], T["po%d" % j][:], "pt%d" % s)
    if rank is not None:
        def count(q):
            hc, j = P["at"][q, rank]
            if hc == core:
                return 1
            return pop(topo.mask(P["ret"][q, rank][0] if (q, rank) in P["ret"] else hc, core))

        def when(q):
            if q == rank:
                return 0
            early = P["at"][q, rank][0] == cores[q]
            return (2.5 if early else 3) if q in P["far"][rank] else 1 if early else 2
        seq = sorted(range(NR), key=when)
        V.wait_ge(S["pt%d" % seq[0]], count(seq[0]))
        for i in range(1, NR):
            V.wait_ge(S["pt%d" % seq[i]], count(seq[i]))
            vw()
            in0 = T["pt%d" % seq[0]][:] if i == 1 else T.acc[:, 0:B]
            if i < NR - 1:
                v(V.tensor_tensor(T.acc[:, 0:B], in0, T["pt%d" % seq[i]][:], A.max))
            else:
                V.tensor_tensor(T.yb[:], in0, T["pt%d" % seq[i]][:], A.max).then_inc(S.yv, 1)
        g.sync.wait_ge(S.yv, 1)
        g.sync.dma_start(T.y[:], T.yb[:]).then_inc(S.yst, 16)
        g.sync.wait_ge(S.yst, 16)
    vw()
    if cnt["loc"]:
        g.wait_ge(S.loc, cnt["loc"])
